import numpy as np
import ml_dtypes


def mxq(x, axis, fmt="e4m3"):
    dtype, down = {"e4m3": (ml_dtypes.float8_e4m3fn, 7), "e5m2": (ml_dtypes.float8_e5m2, 14)}[fmt]
    v = np.moveaxis(np.asarray(x, np.float32).astype(ml_dtypes.bfloat16).astype(np.float64), axis, -1)
    blocks = v.reshape(v.shape[:-1] + (-1, 32))
    amax = np.abs(blocks).max(-1, keepdims=True)
    byte = np.maximum(np.where(amax > 0, np.frexp(amax)[1] - 1 + 127, 0) - down, 1)
    scale = np.exp2(byte - 127.0)
    codes = (blocks / scale).astype(np.float32).astype(dtype).astype(np.float64)
    return np.moveaxis((codes * scale).reshape(v.shape), -1, axis)


WIDE = False


def mx_kscale(k):
    if not WIDE:
        return np.ones(k)
    levels = np.array([10, -10, 5, -5, 0])
    if k % 512:
        return np.exp2(np.random.permutation(np.resize(levels, k // 32))).repeat(32)
    a = np.empty((k // 512, 16))
    for p in range(k // 512):
        a[p, :8] = np.random.permutation(np.resize(levels, 8))
        for g in range(8):
            far = levels[np.abs(levels - a[p, g]) >= 10]
            a[p, g + 8] = far[np.random.randint(len(far))]
    return np.exp2(a.ravel()).repeat(32)


def f64(x):
    return np.asarray(x).astype(np.float64)


def striped(idx):
    return np.tile(idx.reshape(-1, 16).T, (8, 1)).astype(np.uint16)


def unstriped(offs):
    return offs[:16].T.reshape(-1).astype(np.int64)


E2M1 = np.array([0.0, 0.5, 1.0, 1.5, 2.0, 3.0, 4.0, 6.0, -0.0, -0.5, -1.0, -1.5, -2.0, -3.0, -4.0, -6.0])


def pack_weight(w, fmt):
    k, n = w.shape
    w = f64(np.asarray(w, np.float32).astype(ml_dtypes.bfloat16)).reshape(k // 32, 32, n)
    amax = np.abs(w).max(1)
    if fmt == "e4m3":
        byte = np.frexp(amax)[1] - 1 + 127 - 7
    else:
        mant, ex = np.frexp(amax / 6.0)
        byte = np.where(mant > 0.5, ex, ex - 1) + 127
    byte = np.clip(np.where(amax > 0, byte, 1), 1, 254)
    scaled = (w * np.exp2(127.0 - byte)[:, None, :]).reshape(k, n).astype(np.float32)
    by_word = np.ascontiguousarray(scaled.reshape(k // 512, 128, 4, n).transpose(0, 1, 3, 2))
    if fmt == "e4m3":
        words = by_word.astype(ml_dtypes.float8_e4m3fn).view(np.uint8)
    else:
        c = by_word.astype(ml_dtypes.float4_e2m1fn).view(np.uint8) & 0xF
        words = (c[..., 0::2] | (c[..., 1::2] << 4)).reshape(k // 512, 128, 2 * n)
    return np.ascontiguousarray(words), np.ascontiguousarray(byte.astype(np.uint8).reshape(k // 512, 16, n))


def unpack_weight(words, scales, fmt):
    g, _, n = scales.shape
    words = np.ascontiguousarray(words).reshape(g, 128, n, -1)
    if fmt == "e4m3":
        vals = words.view(ml_dtypes.float8_e4m3fn).astype(np.float64)
    else:
        nib = np.empty((g, 128, n, 4), np.uint8)
        nib[..., 0::2] = words & 0xF
        nib[..., 1::2] = words >> 4
        vals = E2M1[nib]
    vals = vals * np.repeat(np.exp2(scales.astype(np.float64) - 127.0), 8, axis=1)[..., None]
    return vals.transpose(0, 1, 3, 2).reshape(g * 512, n)


def gelu(v):
    return 0.5 * v * (1.0 + np.tanh(np.sqrt(2.0 / np.pi) * (v + 0.044715 * v**3)))


def striped8(idx):
    return np.concatenate([v.reshape(-1, 16).T for v in idx]).astype(np.uint16)


def unstriped8(offs):
    return np.stack([offs[16 * g:16 * g + 16].T.reshape(-1) for g in range(8)]).astype(np.int64)


def put_heads(h, wgs, idx8, t2):
    r = np.arange(h.shape[0])
    page = np.zeros((h.shape[0], t2))
    page[r[:, None], idx8[r % 512 // 64]] = wgs[r // 4 % 128] * h
    return page


K, T, S, H, T2, P, N = 1024, 2048, 512, 1024, 1024, 512, 512

def setup_inputs():
    n = np.random.standard_normal
    s = mx_kscale(K)[:, None]
    u = mx_kscale(H)[:, None]
    tab_words, tab_scales = pack_weight(n((K, T)) * s, "e4m3")
    w2_words, w2_scales = pack_weight(0.55 * n((K, H)) / np.sqrt(K) / s, "e2m1")
    w4_words, w4_scales = pack_weight(0.8 * n((H, N)) / np.sqrt(H) / u, "e4m3")
    return {
        "tab_words": tab_words, "tab_scales": tab_scales,
        "offs": striped(np.random.permutation(T)[:S]),
        "w1": (n((K, H)) / np.sqrt(K) / s * u.T).astype(np.float32),
        "w2_words": w2_words, "w2_scales": w2_scales,
        "refr": (0.6 * n((H, S)) * u).astype(np.float32),
        "wgs": np.repeat(np.random.uniform(0.5, 2.0, (8, S)), 16, axis=0).astype(np.float32),
        "offs2": striped8(np.stack([np.random.permutation(T2)[:S] for _ in range(8)])),
        "offs3": striped(np.random.permutation(T2)[:P]),
        "chart": ((0.8 * n((H, P)) - 0.2) * u).astype(np.float32),
        "w3": (1.6 * n((H, N)) / np.sqrt(H) / u).astype(np.float32),
        "w4_words": w4_words, "w4_scales": w4_scales,
    }

def reference(tab_words, tab_scales, offs, w1, w2_words, w2_scales, refr, wgs, offs2, offs3, chart, w3, w4_words, w4_scales):
    v = unpack_weight(tab_words, tab_scales, "e4m3")[:, unstriped(offs)]
    w1q = mxq(f64(w1), 0, "e4m3")
    w2 = unpack_weight(w2_words, w2_scales, "e2m1")
    a = w1q.T @ v
    b = w2.T @ v
    h = a * np.cos(b) + f64(refr)
    page = put_heads(h, f64(wgs), unstriped8(offs2), T2)
    x = page[:, unstriped(offs3)]
    z = mxq(np.maximum(x, f64(chart)), 0, "e4m3")
    w3q = mxq(f64(w3), 0, "e4m3")
    w4 = unpack_weight(w4_words, w4_scales, "e4m3")
    d = w3q.T @ z
    e = w4.T @ z
    y = np.tanh(d) + e
    return y

@@ -1,0 +1,361 @@
+import math
+from contextlib import ExitStack
+
+import concourse.mybir as mybir
+from concourse.masks import make_identity
+
+K, T, S, H, T2, M, N = 1024, 2048, 512, 1024, 1024, 512, 512
+FLOPS = 2 * (2 * K * H * S + 2 * H * N * M)
+
+F32 = mybir.dt.float32
+BF16 = mybir.dt.bfloat16
+I32 = mybir.dt.int32
+U32 = mybir.dt.uint32
+U16 = mybir.dt.uint16
+U8 = mybir.dt.uint8
+FP8X4 = mybir.dt.float8_e4m3fn_x4
+FP4X4 = mybir.dt.float4_e2m1fn_x4
+ACT = mybir.ActivationFunctionType
+ALU = mybir.AluOpType
+
+P = 128
+PACK = 4
+PASS = P * PACK
+SLICES = H // P
+HALF = 256
+
+
+def tile_list_multibeam_bottom_score_kernel(
+    tc, tab_words, tab_scales, offs, w1, w2_words, w2_scales, refr, wgs, offs2, offs3, chart, w3, w4_words, w4_scales, out
+):
+    nc = tc.nc
+    with ExitStack() as ctx:
+        keep = ctx.enter_context(tc.tile_pool(name="keep", bufs=1))
+        ring = ctx.enter_context(tc.tile_pool(name="ring", bufs=2))
+        psum = ctx.enter_context(tc.psum_pool(name="psum", bufs=1))
+
+        def held(shape, dtype, name):
+            return keep.tile(shape, dtype, name=name, align_bytes=64)
+
+        def bank(index, shape, name):
+            return psum.tile(shape, F32, name=name, tag="bank%d" % index)
+
+        idx1 = held([P, S // 16], U16, "idx1")
+        idx2 = held([P, S // 16], U16, "idx2")
+        idx3 = held([P, M // 16], U16, "idx3")
+        tab_w = [held([P, T], I32, "tab_w%d" % a) for a in range(2)]
+        tab_s = held([P, 2 * T], U8, "tab_s")
+        w2_w = [held([P, 2 * 2 * PASS], U8, "w2_w%d" % b) for b in range(2)]
+        w2_s = held([P, 2 * H], U8, "w2_s")
+        w4_w = held([P, 2 * N], I32, "w4_w")
+        w4_s = held([P, 2 * N], U8, "w4_s")
+        v_w = [held([P, S], U32, "v_w%d" % a) for a in range(2)]
+        v_s = [held([P, S], U8, "v_s%d" % a) for a in range(2)]
+        refr_first = held([P, S], F32, "refr_first")
+        refr_rest = held([P, PACK - 1, S], F32, "refr_rest")
+        refr_late = held([P, PACK - 1, S], F32, "refr_late")
+        refr_last = keep.tile([P, S], F32, name="refr_last", tag="last", align_bytes=64)
+        wgs_t = held([P, S], F32, "wgs_t")
+        chart_t = [held([P, PACK, M], F32, "chart%d" % b) for b in range(2)]
+        pages = [held([P, T2], F32, "page%d" % u) for u in range(2)]
+        ident = held([P, P], F32, "ident")
+        shift_h = held([P, SLICES + 1, S], F32, "shift_h")
+        cos_x = held([P, SLICES + 2, S], F32, "cos_x")
+        w1_w = [[held([P, PASS], U32, "w1_w%d%d" % (b, a)) for a in range(2)] for b in range(2)]
+        w1_s = [[held([P, PASS], U8, "w1_s%d%d" % (b, a)) for a in range(2)] for b in range(2)]
+        w3_w = [held([P, N], U32, "w3_w%d" % b) for b in range(2)]
+        w3_s = [held([P, N], U8, "w3_s%d" % b) for b in range(2)]
+        z_w = {(1, u): held([P, HALF], U32, "z_w1%d" % u)[:] for u in range(2)}
+        z_s = [[held([P, HALF], U8, "z_s%d%d" % (b, u)) for u in range(2)] for b in range(2)]
+
+        def load_scales(queue, dst, src):
+            rows = dst[:].bitcast(I32).rearrange("p (a c) -> p a c", a=2)
+            for quad in range(4):
+                queue.dma_start(
+                    out=rows[32 * quad : 32 * quad + 4],
+                    in_=src[:, 4 * quad : 4 * quad + 4, :].bitcast(I32).rearrange("a r c -> r a c"),
+                )
+
+        def load_raw(src, a, c0):
+            raw = ring.tile([P, PACK, HALF], F32, name="raw", tag="raw", bufs=8)
+            rows = src[a * PASS : (a + 1) * PASS, c0 : c0 + HALF]
+            nc.sync.dma_start(out=raw[:], in_=rows.rearrange("(p j) c -> p j c", j=PACK))
+            return raw
+
+        def load_w2(b):
+            nc.sync.dma_start(
+                out=w2_w[b][:].bitcast(I32).rearrange("p (a c) -> p a c", a=2),
+                in_=w2_words[:, :, 2 * PASS * b : 2 * PASS * (b + 1)].bitcast(I32).rearrange("a p c -> p a c"),
+            )
+
+        def load_tab(a):
+            nc.sync.dma_start(out=tab_w[a][:], in_=tab_words[a].rearrange("p t i -> p (t i)").bitcast(I32))
+
+        def by_slice(src, b):
+            return src[b * PASS : (b + 1) * PASS, :].rearrange("(p i) c -> p i c", i=PACK)
+
+        nc.vector.memset(tab_s[:].bitcast(I32), 0)
+        nc.gpsimd.memset(w2_s[:].bitcast(I32), 0)
+        nc.sync.dma_start(idx1[:], offs)
+        load_tab(0)
+        load_scales(nc.sync, tab_s, tab_scales)
+        load_w2(0)
+        load_tab(1)
+        load_scales(nc.gpsimd, w2_s, w2_scales)
+        w1_raw = {}
+        for a in range(2):
+            for u in range(2):
+                w1_raw[0, a, u] = load_raw(w1, a, u * HALF)
+        nc.sync.dma_start(out=refr_first[:], in_=by_slice(refr, 0)[:, 0, :])
+        nc.sync.dma_start(out=wgs_t[:], in_=wgs)
+        nc.sync.dma_start(idx2[:], offs2)
+        nc.sync.dma_start(idx3[:], offs3)
+        nc.sync.dma_start(out=refr_rest[:], in_=by_slice(refr, 0)[:, 1:PACK, :])
+        load_w2(1)
+        for a in range(2):
+            for u in range(2):
+                w1_raw[1, a, u] = load_raw(w1, a, PASS + u * HALF)
+        nc.sync.dma_start(out=refr_late[:], in_=by_slice(refr, 1)[:, 0 : PACK - 1, :])
+        nc.sync.dma_start(out=refr_last[:], in_=by_slice(refr, 1)[:, PACK - 1, :])
+        for page in pages:
+            nc.vector.memset(page[:], 0.0)
+        make_identity(nc, ident[:])
+        nc.vector.memset(w4_s[:].bitcast(I32), 0)
+
+        def gather_words(a, c0, c1):
+            nc.vector.tensor_copy(v_w[a][:, c0:c1], tab_w[a][:].bitcast(U32).indirect(idx1[:, c0 // 16 : c1 // 16]))
+
+        def gather_scales(a):
+            nc.vector.tensor_copy(v_s[a][:], tab_s[:, a * T : (a + 1) * T].indirect(idx1[:]))
+
+        gather_words(0, 0, S)
+        gather_scales(0)
+        gather_scales(1)
+        gather_words(1, 0, HALF)
+        gather_words(1, HALF, S)
+
+        turns = {}
+
+        def phases(b):
+            banks = [bank(jt, [P, PASS], "phase") for jt in range(4)]
+            for a in range(2):
+                for jt in range(4):
+                    cols = slice(jt * P, (jt + 1) * P)
+                    nc.tensor.matmul_mx(
+                        out=banks[jt][:],
+                        lhsT=v_w[a][:, cols].bitcast(FP8X4),
+                        lhsT_scale=v_s[a][:, cols],
+                        rhs=w2_w[b][:, 2 * PASS * a : 2 * PASS * (a + 1)].bitcast(FP4X4),
+                        rhs_scale=w2_s[:, a * H + b * PASS : a * H + (b + 1) * PASS],
+                        start=(a == 0),
+                        stop=(a == 1),
+                    )
+            turns[b] = ring.tile([P, PACK, 4, P], F32, name="turns", tag="turns", align_bytes=64)
+            return banks
+
+        def to_turns(b, banks, jts, i0, i1):
+            for jt in jts:
+                nc.scalar.activation(
+                    turns[b][:, i0:i1, jt, :],
+                    banks[jt][:].rearrange("p (q i) -> p i q", i=PACK)[:, i0:i1, :],
+                    ACT.Abs,
+                    scale=1.0 / (2.0 * math.pi),
+                )
+
+        def staged():
+            return ring.tile([P, PASS * PACK], BF16, name="staged", tag="staged", bufs=3, align_bytes=64)
+
+        def round_w1(copy, b, a):
+            grouped = staged()
+            dst = grouped[:].rearrange("p (i q j) -> p q j i", i=PACK, j=PACK)
+            for u in range(2):
+                copy(
+                    dst[:, u * 64 : (u + 1) * 64],
+                    w1_raw[b, a, u][:].rearrange("p j (q i) -> p q j i", i=PACK),
+                )
+            return grouped
+
+        def quantize(words, scales, grouped, c0, c1):
+            nc.vector.quantize_mx(
+                out=words[:, c0:c1].bitcast(FP8X4), scales=scales[:, c0:c1], in_=grouped[:, PACK * c0 : PACK * c1]
+            )
+
+        echo = {}
+        prod = {}
+
+        def shifts(n, c0, c1):
+            b, i = divmod(n, PACK)
+            whole = ring.tile([P, c1 - c0], U32, name="whole", tag="whole")
+            own = turns[b][:, i].rearrange("p t q -> p (t q)")
+            nc.scalar.activation(whole[:], own[:, c0:c1], ACT.Copy, bias=0.25, scale=1.0)
+            nc.scalar.activation(shift_h[:, n, c0:c1], whole[:], ACT.Copy, bias=0.25, scale=-1.0)
+
+        def cosine(n):
+            b, i = divmod(n, PACK)
+            own = turns[b][:, i].rearrange("p t q -> p (t q)")
+            if n:
+                shifts(n, 0, S)
+            rest = bank(4 + n % 2, [P, S], "rest")
+            for jt in range(4):
+                cols = slice(jt * P, (jt + 1) * P)
+                nc.tensor.matmul(rest[:, cols], own[:, cols], ident[:], start=True, stop=False, is_transpose=True)
+                nc.tensor.matmul(
+                    rest[:, cols], shift_h[:, n, cols], ident[:], start=False, stop=True, is_transpose=True
+                )
+            echo[n] = bank(6 + n % 2, [P, S], "echo")
+            cols = slice(i * P, (i + 1) * P)
+            for a in range(2):
+                nc.tensor.matmul_mx(
+                    out=echo[n][:],
+                    lhsT=w1_w[b][a][:, cols].bitcast(FP8X4),
+                    lhsT_scale=w1_s[b][a][:, cols],
+                    rhs=v_w[a][:].bitcast(FP8X4),
+                    rhs_scale=v_s[a][:],
+                    start=(a == 0),
+                    stop=(a == 1),
+                )
+            nc.scalar.activation(cos_x[:, n, :], rest[:], ACT.Sin, scale=2.0 * math.pi)
+
+        def times_cos(n):
+            prod[n] = ring.tile([P, S], F32, name="prod", tag="prod")
+            nc.vector.tensor_tensor(prod[n][:], echo[n][:], cos_x[:, n, :], ALU.mult)
+
+        def h_slot(n):
+            return shift_h[:, n + 1 if n else 0, :]
+
+        def add_refr(n):
+            b, i = divmod(n, PACK)
+            if n == 0:
+                rows = refr_first[:]
+            elif n == SLICES - 1:
+                rows = refr_last[:]
+            else:
+                rows = refr_late[:, i, :] if b else refr_rest[:, i - 1, :]
+            nc.vector.tensor_tensor(h_slot(n), prod[n][:], rows, ALU.add)
+
+        def scatter(n):
+            nc.vector.tensor_tensor(pages[n % 2][:].indirect(idx2[:]), h_slot(n), wgs_t[:], ALU.mult)
+
+        def fetch(n, u=None):
+            if u is None:
+                nc.vector.tensor_copy(cos_x[:, n + 2, :], pages[n % 2][:].indirect(idx3[:]))
+            else:
+                nc.vector.tensor_copy(
+                    cos_x[:, n + 2, u * HALF : (u + 1) * HALF],
+                    pages[n % 2][:].indirect(idx3[:, u * 16 : (u + 1) * 16]),
+                )
+
+        z_b = {}
+
+        def maximum(b, u):
+            z_b[b, u] = ring.tile([P, HALF * PACK], BF16, name="z_b", tag="z_b", bufs=4, align_bytes=64)
+            cols = slice(u * HALF, (u + 1) * HALF)
+            nc.vector.tensor_tensor(
+                z_b[b, u][:].rearrange("p (c e i) -> p c i e", e=2, i=PACK),
+                cos_x[:, PACK * b + 2 : PACK * b + 6, cols].rearrange("p i (c e) -> p c i e", e=2),
+                chart_t[b][:, :, cols].rearrange("p i (c e) -> p c i e", e=2),
+                ALU.max,
+            )
+
+        def quantize_z(b, u):
+            quantize(z_w[b, u], z_s[b][u], z_b[b, u], 0, HALF)
+
+        def round_w3(b, raws):
+            grouped = staged()
+            dst = grouped[:].rearrange("p (c e j) -> p c j e", e=2, j=PACK)
+            for u in range(2):
+                nc.scalar.copy(
+                    dst[:, u * P : (u + 1) * P], raws[u][:].rearrange("p j (c e) -> p c j e", e=2)
+                )
+            quantize(w3_w[b], w3_s[b], grouped, 0, N)
+
+        score = {}
+
+        def score_pass(b, u):
+            for product, (words, scales, c0) in enumerate(((w3_w[b], w3_s[b], 0), (w4_w, w4_s, b * N))):
+                for nt in range(4):
+                    pair, side = divmod(nt, 2)
+                    if b == 0 and side == 0:
+                        score[product, pair, u] = bank(4 * u + 2 * product + pair, [P, 2, HALF], "score")
+                    cols = slice(c0 + nt * P, c0 + (nt + 1) * P)
+                    nc.tensor.matmul_mx(
+                        out=score[product, pair, u][:, side, :],
+                        lhsT=words[:, cols].bitcast(FP8X4),
+                        lhsT_scale=scales[:, cols],
+                        rhs=z_w[b, u].bitcast(FP8X4),
+                        rhs_scale=z_s[b][u][:],
+                        start=(b == 0 and side == 0),
+                        stop=(b == 1 and side == 1),
+                    )
+
+        def finish(u):
+            for pair in range(2):
+                bent = ring.tile([P, 2, HALF], F32, name="bent", tag="bent")
+                nc.scalar.activation(bent[:], score[0, pair, u][:], ACT.Tanh)
+                for side in range(2):
+                    nt = 2 * pair + side
+                    result = ring.tile([P, HALF], F32, name="result", tag="result", bufs=4)
+                    nc.vector.tensor_tensor(result[:], score[1, pair, u][:, side, :], bent[:, side, :], ALU.add)
+                    nc.sync.dma_start(out=out[nt * P : (nt + 1) * P, u * HALF : (u + 1) * HALF], in_=result[:])
+
+        banks = phases(0)
+        for u in range(2):
+            to_turns(0, banks, (2 * u, 2 * u + 1), 0, 1)
+            shifts(0, u * HALF, (u + 1) * HALF)
+        grouped = round_w1(nc.vector.tensor_copy, 0, 0)
+        quantize(w1_w[0][0], w1_s[0][0], grouped, 0, PASS)
+        grouped = round_w1(nc.vector.tensor_copy, 0, 1)
+        quantize(w1_w[0][1], w1_s[0][1], grouped, 0, P)
+        quantize(w1_w[0][1], w1_s[0][1], grouped, P, PASS)
+
+        w3_raw = [[load_raw(w3, b, u * HALF) for u in range(2)] for b in range(2)]
+        nc.sync.dma_start(out=chart_t[0][:], in_=by_slice(chart, 0))
+        nc.sync.dma_start(
+            out=w4_w[:].rearrange("p (a c) -> p a c", a=2),
+            in_=w4_words.rearrange("a p c i -> p a (c i)").bitcast(I32),
+        )
+        load_scales(nc.sync, w4_s, w4_scales)
+        nc.sync.dma_start(out=chart_t[1][:], in_=by_slice(chart, 1))
+
+        cosine(0)
+        to_turns(0, banks, range(4), 1, PACK)
+        times_cos(0)
+        add_refr(0)
+        scatter(0)
+        cosine(1)
+        times_cos(1)
+        for n in range(1, SLICES):
+            if n + 1 < SLICES:
+                cosine(n + 1)
+            add_refr(n)
+            if n + 1 < SLICES:
+                times_cos(n + 1)
+            if n + 1 == SLICES:
+                fetch(n - 1)
+            scatter(n)
+            if n + 1 < SLICES:
+                fetch(n - 1)
+            if n == 2:
+                for a in range(2):
+                    grouped = round_w1(nc.scalar.copy, 1, a)
+                    quantize(w1_w[1][a], w1_s[1][a], grouped, 0, PASS)
+                to_turns(1, phases(1), range(4), 0, PACK)
+            if n == 4:
+                for u in range(2):
+                    maximum(0, u)
+                for b in range(2):
+                    round_w3(b, w3_raw[b])
+        first_words = keep.tile([P, M], U32, name="first_words", tag="last", align_bytes=64)
+        for u in range(2):
+            z_w[0, u] = first_words[:, u * HALF : (u + 1) * HALF]
+            quantize_z(0, u)
+        for u in range(2):
+            score_pass(0, u)
+        for u in range(2):
+            fetch(SLICES - 1, u)
+        for u in range(2):
+            maximum(1, u)
+            quantize_z(1, u)
+        for u in range(2):
+            score_pass(1, u)
+            finish(u)

@@ -55,7 +55,7 @@ def tile_list_multibeam_bottom_score_kernel(
         refr_rest = held([P, PACK - 1, S], F32, "refr_rest")
         refr_late = held([P, PACK - 1, S], F32, "refr_late")
         refr_last = keep.tile([P, S], F32, name="refr_last", tag="last", align_bytes=64)
-        wgs_t = held([P, S], F32, "wgs_t")
+        wgs_t = keep.tile([P, S], F32, name="wgs_t", tag="weights", align_bytes=64)
         chart_t = [held([P, PACK, M], F32, "chart%d" % b) for b in range(2)]
         pages = [held([P, T2], F32, "page%d" % u) for u in range(2)]
         ident = held([P, P], F32, "ident")
@@ -68,10 +68,10 @@ def tile_list_multibeam_bottom_score_kernel(
         z_w = {(1, u): held([P, HALF], U32, "z_w1%d" % u)[:] for u in range(2)}
         z_s = [[held([P, HALF], U8, "z_s%d%d" % (b, u)) for u in range(2)] for b in range(2)]
 
-        def load_scales(queue, dst, src):
+        def load_scales(dst, src):
             rows = dst[:].bitcast(I32).rearrange("p (a c) -> p a c", a=2)
             for quad in range(4):
-                queue.dma_start(
+                nc.sync.dma_start(
                     out=rows[32 * quad : 32 * quad + 4],
                     in_=src[:, 4 * quad : 4 * quad + 4, :].bitcast(I32).rearrange("a r c -> r a c"),
                 )
@@ -94,14 +94,16 @@ def tile_list_multibeam_bottom_score_kernel(
         def by_slice(src, b):
             return src[b * PASS : (b + 1) * PASS, :].rearrange("(p i) c -> p i c", i=PACK)
 
-        nc.vector.memset(tab_s[:].bitcast(I32), 0)
-        nc.gpsimd.memset(w2_s[:].bitcast(I32), 0)
+        nc.gpsimd.memset(tab_s[:, 0:T].bitcast(I32), 0)
+        nc.vector.memset(tab_s[:, T : 2 * T].bitcast(I32), 0)
+        nc.vector.memset(w2_s[:].bitcast(I32), 0)
+        nc.gpsimd.memset(w4_s[:].bitcast(I32), 0)
         nc.sync.dma_start(idx1[:], offs)
+        load_scales(tab_s, tab_scales)
         load_tab(0)
-        load_scales(nc.sync, tab_s, tab_scales)
         load_w2(0)
+        load_scales(w2_s, w2_scales)
         load_tab(1)
-        load_scales(nc.gpsimd, w2_s, w2_scales)
         w1_raw = {}
         for a in range(2):
             for u in range(2):
@@ -120,7 +122,6 @@ def tile_list_multibeam_bottom_score_kernel(
         for page in pages:
             nc.vector.memset(page[:], 0.0)
         make_identity(nc, ident[:])
-        nc.vector.memset(w4_s[:].bitcast(I32), 0)
 
         def gather_words(a, c0, c1):
             nc.vector.tensor_copy(v_w[a][:, c0:c1], tab_w[a][:].bitcast(U32).indirect(idx1[:, c0 // 16 : c1 // 16]))
@@ -128,9 +129,9 @@ def tile_list_multibeam_bottom_score_kernel(
         def gather_scales(a):
             nc.vector.tensor_copy(v_s[a][:], tab_s[:, a * T : (a + 1) * T].indirect(idx1[:]))
 
-        gather_words(0, 0, S)
         gather_scales(0)
         gather_scales(1)
+        gather_words(0, 0, S)
         gather_words(1, 0, HALF)
         gather_words(1, HALF, S)
 
@@ -290,13 +291,12 @@ def tile_list_multibeam_bottom_score_kernel(
 
         def finish(u):
             for pair in range(2):
-                bent = ring.tile([P, 2, HALF], F32, name="bent", tag="bent")
+                bent = ring.tile([P, 2, HALF], F32, name="bent", tag="bent", bufs=3)
                 nc.scalar.activation(bent[:], score[0, pair, u][:], ACT.Tanh)
-                for side in range(2):
-                    nt = 2 * pair + side
-                    result = ring.tile([P, HALF], F32, name="result", tag="result", bufs=4)
-                    nc.vector.tensor_tensor(result[:], score[1, pair, u][:, side, :], bent[:, side, :], ALU.add)
-                    nc.sync.dma_start(out=out[nt * P : (nt + 1) * P, u * HALF : (u + 1) * HALF], in_=result[:])
+                result = ring.tile([P, 2, HALF], F32, name="result", tag="result", bufs=4)
+                nc.vector.tensor_tensor(result[:], score[1, pair, u][:], bent[:], ALU.add)
+                rows = out[2 * pair * P : 2 * (pair + 1) * P, u * HALF : (u + 1) * HALF]
+                nc.sync.dma_start(out=rows.rearrange("(s p) c -> p s c", p=P), in_=result[:])
 
         banks = phases(0)
         for u in range(2):
@@ -314,7 +314,7 @@ def tile_list_multibeam_bottom_score_kernel(
             out=w4_w[:].rearrange("p (a c) -> p a c", a=2),
             in_=w4_words.rearrange("a p c i -> p a (c i)").bitcast(I32),
         )
-        load_scales(nc.sync, w4_s, w4_scales)
+        load_scales(w4_s, w4_scales)
         nc.sync.dma_start(out=chart_t[1][:], in_=by_slice(chart, 1))
 
         cosine(0)
@@ -345,17 +345,18 @@ def tile_list_multibeam_bottom_score_kernel(
                     maximum(0, u)
                 for b in range(2):
                     round_w3(b, w3_raw[b])
-        first_words = keep.tile([P, M], U32, name="first_words", tag="last", align_bytes=64)
-        for u in range(2):
-            z_w[0, u] = first_words[:, u * HALF : (u + 1) * HALF]
-            quantize_z(0, u)
-        for u in range(2):
-            score_pass(0, u)
+        for u, tag in enumerate(("last", "weights")):
+            z_w[0, u] = keep.tile([P, HALF], U32, name="first_words", tag=tag, align_bytes=64)[:]
+        quantize_z(0, 0)
+        score_pass(0, 0)
         for u in range(2):
             fetch(SLICES - 1, u)
-        for u in range(2):
-            maximum(1, u)
-            quantize_z(1, u)
+        maximum(1, 0)
+        quantize_z(0, 1)
+        quantize_z(1, 0)
+        maximum(1, 1)
+        quantize_z(1, 1)
+        score_pass(0, 1)
         for u in range(2):
             score_pass(1, u)
             finish(u)

@@ -94,6 +94,10 @@ def tile_list_multibeam_bottom_score_kernel(
         def by_slice(src, b):
             return src[b * PASS : (b + 1) * PASS, :].rearrange("(p i) c -> p i c", i=PACK)
 
+        warm_in = held([P, 8], F32, "warm_in")
+        warm_out = held([P, 8], F32, "warm_out")
+        nc.vector.memset(warm_in[:], 0.0)
+        nc.scalar.activation(warm_out[:], warm_in[:], ACT.Silu)
         nc.gpsimd.memset(tab_s[:, 0:T].bitcast(I32), 0)
         nc.vector.memset(tab_s[:, T : 2 * T].bitcast(I32), 0)
         nc.vector.memset(w2_s[:].bitcast(I32), 0)

import math
from contextlib import ExitStack

import concourse.mybir as mybir
from concourse.masks import make_identity

K, T, S, H, T2, M, N = 1024, 2048, 512, 1024, 1024, 512, 512
FLOPS = 2 * (2 * K * H * S + 2 * H * N * M)

F32 = mybir.dt.float32
BF16 = mybir.dt.bfloat16
I32 = mybir.dt.int32
U32 = mybir.dt.uint32
U16 = mybir.dt.uint16
U8 = mybir.dt.uint8
FP8X4 = mybir.dt.float8_e4m3fn_x4
FP4X4 = mybir.dt.float4_e2m1fn_x4
ACT = mybir.ActivationFunctionType
ALU = mybir.AluOpType

P = 128
PACK = 4
PASS = P * PACK
SLICES = H // P
HALF = 256


def tile_list_multibeam_bottom_score_kernel(
    tc, tab_words, tab_scales, offs, w1, w2_words, w2_scales, refr, wgs, offs2, offs3, chart, w3, w4_words, w4_scales, out
):
    nc = tc.nc
    with ExitStack() as ctx:
        keep = ctx.enter_context(tc.tile_pool(name="keep", bufs=1))
        ring = ctx.enter_context(tc.tile_pool(name="ring", bufs=2))
        psum = ctx.enter_context(tc.psum_pool(name="psum", bufs=1))

        def held(shape, dtype, name):
            return keep.tile(shape, dtype, name=name, align_bytes=64)

        def bank(index, shape, name):
            return psum.tile(shape, F32, name=name, tag="bank%d" % index)

        idx1 = held([P, S // 16], U16, "idx1")
        idx2 = held([P, S // 16], U16, "idx2")
        idx3 = held([P, M // 16], U16, "idx3")
        tab_w = [held([P, T], I32, "tab_w%d" % a) for a in range(2)]
        tab_s = held([P, 2 * T], U8, "tab_s")
        w2_w = [held([P, 2 * 2 * PASS], U8, "w2_w%d" % b) for b in range(2)]
        w2_s = held([P, 2 * H], U8, "w2_s")
        w4_w = held([P, 2 * N], I32, "w4_w")
        w4_s = held([P, 2 * N], U8, "w4_s")
        v_w = [held([P, S], U32, "v_w%d" % a) for a in range(2)]
        v_s = [held([P, S], U8, "v_s%d" % a) for a in range(2)]
        refr_first = held([P, S], F32, "refr_first")
        refr_rest = held([P, PACK - 1, S], F32, "refr_rest")
        refr_late = held([P, PACK - 1, S], F32, "refr_late")
        refr_last = keep.tile([P, S], F32, name="refr_last", tag="last", align_bytes=64)
        wgs_t = keep.tile([P, S], F32, name="wgs_t", tag="weights", align_bytes=64)
        chart_t = [held([P, PACK, M], F32, "chart%d" % b) for b in range(2)]
        pages = [held([P, T2], F32, "page%d" % u) for u in range(2)]
        ident = held([P, P], F32, "ident")
        shift_h = held([P, SLICES + 1, S], F32, "shift_h")
        cos_x = held([P, SLICES + 2, S], F32, "cos_x")
        w1_w = [[held([P, PASS], U32, "w1_w%d%d" % (b, a)) for a in range(2)] for b in range(2)]
        w1_s = [[held([P, PASS], U8, "w1_s%d%d" % (b, a)) for a in range(2)] for b in range(2)]
        w3_w = [held([P, N], U32, "w3_w%d" % b) for b in range(2)]
        w3_s = [held([P, N], U8, "w3_s%d" % b) for b in range(2)]
        z_w = {(1, u): held([P, HALF], U32, "z_w1%d" % u)[:] for u in range(2)}
        z_s = [[held([P, HALF], U8, "z_s%d%d" % (b, u)) for u in range(2)] for b in range(2)]

        def load_scales(dst, src):
            rows = dst[:].bitcast(I32).rearrange("p (a c) -> p a c", a=2)
            for quad in range(4):
                nc.sync.dma_start(
                    out=rows[32 * quad : 32 * quad + 4],
                    in_=src[:, 4 * quad : 4 * quad + 4, :].bitcast(I32).rearrange("a r c -> r a c"),
                )

        def load_raw(src, a, c0):
            raw = ring.tile([P, PACK, HALF], F32, name="raw", tag="raw", bufs=8)
            rows = src[a * PASS : (a + 1) * PASS, c0 : c0 + HALF]
            nc.sync.dma_start(out=raw[:], in_=rows.rearrange("(p j) c -> p j c", j=PACK))
            return raw

        def load_w2(b):
            nc.sync.dma_start(
                out=w2_w[b][:].bitcast(I32).rearrange("p (a c) -> p a c", a=2),
                in_=w2_words[:, :, 2 * PASS * b : 2 * PASS * (b + 1)].bitcast(I32).rearrange("a p c -> p a c"),
            )

        def load_tab(a):
            nc.sync.dma_start(out=tab_w[a][:], in_=tab_words[a].rearrange("p t i -> p (t i)").bitcast(I32))

        def by_slice(src, b):
            return src[b * PASS : (b + 1) * PASS, :].rearrange("(p i) c -> p i c", i=PACK)

        warm_in = held([P, 8], F32, "warm_in")
        warm_out = held([P, 8], F32, "warm_out")
        nc.vector.memset(warm_in[:], 0.0)
        nc.scalar.activation(warm_out[:], warm_in[:], ACT.Silu)
        nc.gpsimd.memset(tab_s[:, 0:T].bitcast(I32), 0)
        nc.vector.memset(tab_s[:, T : 2 * T].bitcast(I32), 0)
        nc.vector.memset(w2_s[:].bitcast(I32), 0)
        nc.gpsimd.memset(w4_s[:].bitcast(I32), 0)
        nc.sync.dma_start(idx1[:], offs)
        load_scales(tab_s, tab_scales)
        load_tab(0)
        load_w2(0)
        load_scales(w2_s, w2_scales)
        load_tab(1)
        w1_raw = {}
        for a in range(2):
            for u in range(2):
                w1_raw[0, a, u] = load_raw(w1, a, u * HALF)
        nc.sync.dma_start(out=refr_first[:], in_=by_slice(refr, 0)[:, 0, :])
        nc.sync.dma_start(out=wgs_t[:], in_=wgs)
        nc.sync.dma_start(idx2[:], offs2)
        nc.sync.dma_start(idx3[:], offs3)
        nc.sync.dma_start(out=refr_rest[:], in_=by_slice(refr, 0)[:, 1:PACK, :])
        load_w2(1)
        for a in range(2):
            for u in range(2):
                w1_raw[1, a, u] = load_raw(w1, a, PASS + u * HALF)
        nc.sync.dma_start(out=refr_late[:], in_=by_slice(refr, 1)[:, 0 : PACK - 1, :])
        nc.sync.dma_start(out=refr_last[:], in_=by_slice(refr, 1)[:, PACK - 1, :])
        for page in pages:
            nc.vector.memset(page[:], 0.0)
        make_identity(nc, ident[:])

        def gather_words(a, c0, c1):
            nc.vector.tensor_copy(v_w[a][:, c0:c1], tab_w[a][:].bitcast(U32).indirect(idx1[:, c0 // 16 : c1 // 16]))

        def gather_scales(a):
            nc.vector.tensor_copy(v_s[a][:], tab_s[:, a * T : (a + 1) * T].indirect(idx1[:]))

        gather_scales(0)
        gather_scales(1)
        gather_words(0, 0, S)
        gather_words(1, 0, HALF)
        gather_words(1, HALF, S)

        turns = {}

        def phases(b):
            banks = [bank(jt, [P, PASS], "phase") for jt in range(4)]
            for a in range(2):
                for jt in range(4):
                    cols = slice(jt * P, (jt + 1) * P)
                    nc.tensor.matmul_mx(
                        out=banks[jt][:],
                        lhsT=v_w[a][:, cols].bitcast(FP8X4),
                        lhsT_scale=v_s[a][:, cols],
                        rhs=w2_w[b][:, 2 * PASS * a : 2 * PASS * (a + 1)].bitcast(FP4X4),
                        rhs_scale=w2_s[:, a * H + b * PASS : a * H + (b + 1) * PASS],
                        start=(a == 0),
                        stop=(a == 1),
                    )
            turns[b] = ring.tile([P, PACK, 4, P], F32, name="turns", tag="turns", align_bytes=64)
            return banks

        def to_turns(b, banks, jts, i0, i1):
            for jt in jts:
                nc.scalar.activation(
                    turns[b][:, i0:i1, jt, :],
                    banks[jt][:].rearrange("p (q i) -> p i q", i=PACK)[:, i0:i1, :],
                    ACT.Abs,
                    scale=1.0 / (2.0 * math.pi),
                )

        def staged():
            return ring.tile([P, PASS * PACK], BF16, name="staged", tag="staged", bufs=3, align_bytes=64)

        def round_w1(copy, b, a):
            grouped = staged()
            dst = grouped[:].rearrange("p (i q j) -> p q j i", i=PACK, j=PACK)
            for u in range(2):
                copy(
                    dst[:, u * 64 : (u + 1) * 64],
                    w1_raw[b, a, u][:].rearrange("p j (q i) -> p q j i", i=PACK),
                )
            return grouped

        def quantize(words, scales, grouped, c0, c1):
            nc.vector.quantize_mx(
                out=words[:, c0:c1].bitcast(FP8X4), scales=scales[:, c0:c1], in_=grouped[:, PACK * c0 : PACK * c1]
            )

        echo = {}
        prod = {}

        def shifts(n, c0, c1):
            b, i = divmod(n, PACK)
            whole = ring.tile([P, c1 - c0], U32, name="whole", tag="whole")
            own = turns[b][:, i].rearrange("p t q -> p (t q)")
            nc.scalar.activation(whole[:], own[:, c0:c1], ACT.Copy, bias=0.25, scale=1.0)
            nc.scalar.activation(shift_h[:, n, c0:c1], whole[:], ACT.Copy, bias=0.25, scale=-1.0)

        def cosine(n):
            b, i = divmod(n, PACK)
            own = turns[b][:, i].rearrange("p t q -> p (t q)")
            if n:
                shifts(n, 0, S)
            rest = bank(4 + n % 2, [P, S], "rest")
            for jt in range(4):
                cols = slice(jt * P, (jt + 1) * P)
                nc.tensor.matmul(rest[:, cols], own[:, cols], ident[:], start=True, stop=False, is_transpose=True)
                nc.tensor.matmul(
                    rest[:, cols], shift_h[:, n, cols], ident[:], start=False, stop=True, is_transpose=True
                )
            echo[n] = bank(6 + n % 2, [P, S], "echo")
            cols = slice(i * P, (i + 1) * P)
            for a in range(2):
                nc.tensor.matmul_mx(
                    out=echo[n][:],
                    lhsT=w1_w[b][a][:, cols].bitcast(FP8X4),
                    lhsT_scale=w1_s[b][a][:, cols],
                    rhs=v_w[a][:].bitcast(FP8X4),
                    rhs_scale=v_s[a][:],
                    start=(a == 0),
                    stop=(a == 1),
                )
            nc.scalar.activation(cos_x[:, n, :], rest[:], ACT.Sin, scale=2.0 * math.pi)

        def times_cos(n):
            prod[n] = ring.tile([P, S], F32, name="prod", tag="prod")
            nc.vector.tensor_tensor(prod[n][:], echo[n][:], cos_x[:, n, :], ALU.mult)

        def h_slot(n):
            return shift_h[:, n + 1 if n else 0, :]

        def add_refr(n):
            b, i = divmod(n, PACK)
            if n == 0:
                rows = refr_first[:]
            elif n == SLICES - 1:
                rows = refr_last[:]
            else:
                rows = refr_late[:, i, :] if b else refr_rest[:, i - 1, :]
            nc.vector.tensor_tensor(h_slot(n), prod[n][:], rows, ALU.add)

        def scatter(n):
            nc.vector.tensor_tensor(pages[n % 2][:].indirect(idx2[:]), h_slot(n), wgs_t[:], ALU.mult)

        def fetch(n, u=None):
            if u is None:
                nc.vector.tensor_copy(cos_x[:, n + 2, :], pages[n % 2][:].indirect(idx3[:]))
            else:
                nc.vector.tensor_copy(
                    cos_x[:, n + 2, u * HALF : (u + 1) * HALF],
                    pages[n % 2][:].indirect(idx3[:, u * 16 : (u + 1) * 16]),
                )

        z_b = {}

        def maximum(b, u):
            z_b[b, u] = ring.tile([P, HALF * PACK], BF16, name="z_b", tag="z_b", bufs=4, align_bytes=64)
            cols = slice(u * HALF, (u + 1) * HALF)
            nc.vector.tensor_tensor(
                z_b[b, u][:].rearrange("p (c e i) -> p c i e", e=2, i=PACK),
                cos_x[:, PACK * b + 2 : PACK * b + 6, cols].rearrange("p i (c e) -> p c i e", e=2),
                chart_t[b][:, :, cols].rearrange("p i (c e) -> p c i e", e=2),
                ALU.max,
            )

        def quantize_z(b, u):
            quantize(z_w[b, u], z_s[b][u], z_b[b, u], 0, HALF)

        def round_w3(b, raws):
            grouped = staged()
            dst = grouped[:].rearrange("p (c e j) -> p c j e", e=2, j=PACK)
            for u in range(2):
                nc.scalar.copy(
                    dst[:, u * P : (u + 1) * P], raws[u][:].rearrange("p j (c e) -> p c j e", e=2)
                )
            quantize(w3_w[b], w3_s[b], grouped, 0, N)

        score = {}

        def score_pass(b, u):
            for product, (words, scales, c0) in enumerate(((w3_w[b], w3_s[b], 0), (w4_w, w4_s, b * N))):
                for nt in range(4):
                    pair, side = divmod(nt, 2)
                    if b == 0 and side == 0:
                        score[product, pair, u] = bank(4 * u + 2 * product + pair, [P, 2, HALF], "score")
                    cols = slice(c0 + nt * P, c0 + (nt + 1) * P)
                    nc.tensor.matmul_mx(
                        out=score[product, pair, u][:, side, :],
                        lhsT=words[:, cols].bitcast(FP8X4),
                        lhsT_scale=scales[:, cols],
                        rhs=z_w[b, u].bitcast(FP8X4),
                        rhs_scale=z_s[b][u][:],
                        start=(b == 0 and side == 0),
                        stop=(b == 1 and side == 1),
                    )

        def finish(u):
            for pair in range(2):
                bent = ring.tile([P, 2, HALF], F32, name="bent", tag="bent", bufs=3)
                nc.scalar.activation(bent[:], score[0, pair, u][:], ACT.Tanh)
                result = ring.tile([P, 2, HALF], F32, name="result", tag="result", bufs=4)
                nc.vector.tensor_tensor(result[:], score[1, pair, u][:], bent[:], ALU.add)
                rows = out[2 * pair * P : 2 * (pair + 1) * P, u * HALF : (u + 1) * HALF]
                nc.sync.dma_start(out=rows.rearrange("(s p) c -> p s c", p=P), in_=result[:])

        banks = phases(0)
        for u in range(2):
            to_turns(0, banks, (2 * u, 2 * u + 1), 0, 1)
            shifts(0, u * HALF, (u + 1) * HALF)
        grouped = round_w1(nc.vector.tensor_copy, 0, 0)
        quantize(w1_w[0][0], w1_s[0][0], grouped, 0, PASS)
        grouped = round_w1(nc.vector.tensor_copy, 0, 1)
        quantize(w1_w[0][1], w1_s[0][1], grouped, 0, P)
        quantize(w1_w[0][1], w1_s[0][1], grouped, P, PASS)

        w3_raw = [[load_raw(w3, b, u * HALF) for u in range(2)] for b in range(2)]
        nc.sync.dma_start(out=chart_t[0][:], in_=by_slice(chart, 0))
        nc.sync.dma_start(
            out=w4_w[:].rearrange("p (a c) -> p a c", a=2),
            in_=w4_words.rearrange("a p c i -> p a (c i)").bitcast(I32),
        )
        load_scales(w4_s, w4_scales)
        nc.sync.dma_start(out=chart_t[1][:], in_=by_slice(chart, 1))

        cosine(0)
        to_turns(0, banks, range(4), 1, PACK)
        times_cos(0)
        add_refr(0)
        scatter(0)
        cosine(1)
        times_cos(1)
        for n in range(1, SLICES):
            if n + 1 < SLICES:
                cosine(n + 1)
            add_refr(n)
            if n + 1 < SLICES:
                times_cos(n + 1)
            if n + 1 == SLICES:
                fetch(n - 1)
            scatter(n)
            if n + 1 < SLICES:
                fetch(n - 1)
            if n == 2:
                for a in range(2):
                    grouped = round_w1(nc.scalar.copy, 1, a)
                    quantize(w1_w[1][a], w1_s[1][a], grouped, 0, PASS)
                to_turns(1, phases(1), range(4), 0, PACK)
            if n == 4:
                for u in range(2):
                    maximum(0, u)
                for b in range(2):
                    round_w3(b, w3_raw[b])
        for u, tag in enumerate(("last", "weights")):
            z_w[0, u] = keep.tile([P, HALF], U32, name="first_words", tag=tag, align_bytes=64)[:]
        quantize_z(0, 0)
        score_pass(0, 0)
        for u in range(2):
            fetch(SLICES - 1, u)
        maximum(1, 0)
        quantize_z(0, 1)
        quantize_z(1, 0)
        maximum(1, 1)
        quantize_z(1, 1)
        score_pass(0, 1)
        for u in range(2):
            score_pass(1, u)
            finish(u)
